import numpy as np
import ml_dtypes

BF16 = ml_dtypes.bfloat16


def bf(x):
    return np.asarray(x, np.float32).astype(BF16)


def f32(x):
    return np.asarray(x, np.float32)


def f64(x):
    return np.asarray(x).astype(np.float64)


def striped(idx):
    return np.tile(idx.reshape(-1, 16).T, (8, 1))


def rows(idx, k):
    return np.tile(idx, (k, 1))


def look(tab, idx):
    return np.take_along_axis(f64(tab), rows(idx, len(tab)), axis=1)


K, S, H, V, N = 256, 2048, 256, 1024, 1024


def setup_inputs():
    return {"z": bf(np.random.standard_normal((H, S))), "wt": bf(np.random.standard_normal((H, K)) / np.sqrt(H)), "y": f32(1.0 * np.random.standard_normal((K, V))), "offs": striped(np.random.permutation(S)[:N])}


def reference(z, wt, y, offs):
    idx = offs[:16].T.reshape(-1)
    tab = f64(wt).T @ f64(z)
    x = f64(y) / (1.0 + np.exp(-look(tab, idx)))
    return x

@@ -1,0 +1,60 @@
+import concourse.mybir as mybir
+
+P = 128
+BANK = 512
+GROUP = 16
+PIECE = 512
+
+FLOPS = 2 * 256 * 256 * 2048
+
+BF16, F32, U16 = mybir.dt.bfloat16, mybir.dt.float32, mybir.dt.uint16
+SIGMOID = mybir.ActivationFunctionType.Sigmoid
+MULT = mybir.AluOpType.mult
+
+
+def tile_lookup_pjsig_out_kernel(tc, z, wt, y, offs, out):
+    nc = tc.nc
+    features, places = z.shape
+    rows, entries = y.shape
+    halves, blocks, chunks = features // P, rows // P, places // BANK
+
+    z_split = z.rearrange("(p h) s -> p h s", h=halves)
+    wt_split = wt.rearrange("(p h) r -> p h r", h=halves)
+
+    with (
+        tc.tile_pool(name="held", bufs=1) as held,
+        tc.psum_pool(name="psum", bufs=1) as psum,
+    ):
+        weights = held.tile([P, halves, rows], BF16, name="weights")
+        nc.scalar.dma_start(weights[:], wt_split)
+        feats = [held.tile([P, halves, BANK], BF16, name=f"feats{c}") for c in range(chunks)]
+        for c in range(chunks):
+            nc.sync.dma_start(feats[c][:], z_split[:, :, c * BANK : (c + 1) * BANK])
+        offsets = held.tile([P, entries // GROUP], U16, name="offsets")
+        nc.sync.dma_start(offsets[:], offs)
+        stream = [held.tile([P, entries], F32, name=f"stream{b}") for b in range(blocks)]
+        for b in range(blocks):
+            nc.sync.dma_start(stream[b][:], y[b * P : (b + 1) * P, :])
+
+        table = [held.tile([P, places], F32, name=f"table{b}") for b in range(blocks)]
+        for b in range(blocks):
+            for c in range(chunks):
+                scores = psum.tile([P, BANK], F32, name=f"scores{b}_{c}")
+                for h in range(halves):
+                    nc.tensor.matmul(scores[:], weights[:, h, b * P : (b + 1) * P], feats[c][:, h, :],
+                                     start=(h == 0), stop=(h == halves - 1))
+                columns = table[b][:, c * BANK : (c + 1) * BANK]
+                if b == 0 and c % 2 == 1:
+                    nc.scalar.copy(columns, scores[:])
+                else:
+                    nc.vector.tensor_copy(columns, scores[:])
+
+        for b in range(blocks):
+            gate = held.tile([P, entries], F32, name=f"gate{b}")
+            gated = held.tile([P, entries], F32, name=f"gated{b}")
+            for start in range(0, entries, PIECE):
+                piece = slice(start, start + PIECE)
+                listed = offsets[:, start // GROUP : (start + PIECE) // GROUP]
+                nc.scalar.activation(gate[:, piece], table[b][:].indirect(listed), SIGMOID)
+                nc.vector.tensor_tensor(gated[:, piece], gate[:, piece], stream[b][:, piece], MULT)
+                nc.sync.dma_start(out[b * P : (b + 1) * P, piece], gated[:, piece])

@@ -3,7 +3,10 @@ import concourse.mybir as mybir
 P = 128
 BANK = 512
 GROUP = 16
-PIECE = 512
+SMALLEST = 128
+BANKS = 8
+WARM_MATMULS = 6
+WARM_WIDTH = 256
 
 FLOPS = 2 * 256 * 256 * 2048
 
@@ -12,38 +15,57 @@ SIGMOID = mybir.ActivationFunctionType.Sigmoid
 MULT = mybir.AluOpType.mult
 
 
+def halving(total, smallest):
+    pieces, start = [], 0
+    while total - start > smallest:
+        width = (total - start) // 2
+        pieces.append(slice(start, start + width))
+        start += width
+    return pieces + [slice(start, total)]
+
+
 def tile_lookup_pjsig_out_kernel(tc, z, wt, y, offs, out):
     nc = tc.nc
     features, places = z.shape
     rows, entries = y.shape
-    halves, blocks, chunks = features // P, rows // P, places // BANK
+    halves, blocks = features // P, rows // P
+    edges = [0] + list(range(BANK // 2, places, BANK)) + [places]
+    chunks = [slice(lo, hi) for lo, hi in zip(edges, edges[1:])]
 
     z_split = z.rearrange("(p h) s -> p h s", h=halves)
     wt_split = wt.rearrange("(p h) r -> p h r", h=halves)
 
     with (
         tc.tile_pool(name="held", bufs=1) as held,
-        tc.psum_pool(name="psum", bufs=1) as psum,
+        tc.psum_pool(name="psum", bufs=BANKS) as psum,
     ):
         weights = held.tile([P, halves, rows], BF16, name="weights")
         nc.scalar.dma_start(weights[:], wt_split)
-        feats = [held.tile([P, halves, BANK], BF16, name=f"feats{c}") for c in range(chunks)]
-        for c in range(chunks):
-            nc.sync.dma_start(feats[c][:], z_split[:, :, c * BANK : (c + 1) * BANK])
+        feats = held.tile([P, halves, places], BF16, name="feats")
+        for chunk in chunks:
+            nc.sync.dma_start(feats[:, :, chunk], z_split[:, :, chunk])
         offsets = held.tile([P, entries // GROUP], U16, name="offsets")
         nc.sync.dma_start(offsets[:], offs)
-        stream = [held.tile([P, entries], F32, name=f"stream{b}") for b in range(blocks)]
-        for b in range(blocks):
-            nc.sync.dma_start(stream[b][:], y[b * P : (b + 1) * P, :])
+
+        zeros = held.tile([P, WARM_WIDTH], BF16, name="zeros", tag="late")
+        nc.vector.memset(zeros[:], 0.0)
+        unused_gate = held.tile([P, 1], F32, name="unused_gate")
+        nc.scalar.activation(unused_gate[:], zeros[:, 0:1], SIGMOID)
+        unused_scores = psum.tile([P, WARM_WIDTH], F32, name="unused_scores", tag="bank")
+        for w in range(WARM_MATMULS):
+            nc.tensor.matmul(unused_scores[:], zeros[:, 0:P], zeros[:], start=True, stop=True)
+
+        stream = held.tile([P, blocks, entries], F32, name="stream", tag="late")
+        nc.sync.dma_start(stream[:], y.rearrange("(b p) j -> p b j", p=P))
 
         table = [held.tile([P, places], F32, name=f"table{b}") for b in range(blocks)]
         for b in range(blocks):
-            for c in range(chunks):
-                scores = psum.tile([P, BANK], F32, name=f"scores{b}_{c}")
+            for c, chunk in enumerate(chunks):
+                scores = psum.tile([P, chunk.stop - chunk.start], F32, name=f"scores{b}_{c}", tag="bank")
                 for h in range(halves):
-                    nc.tensor.matmul(scores[:], weights[:, h, b * P : (b + 1) * P], feats[c][:, h, :],
+                    nc.tensor.matmul(scores[:], weights[:, h, b * P : (b + 1) * P], feats[:, h, chunk],
                                      start=(h == 0), stop=(h == halves - 1))
-                columns = table[b][:, c * BANK : (c + 1) * BANK]
+                columns = table[b][:, chunk]
                 if b == 0 and c % 2 == 1:
                     nc.scalar.copy(columns, scores[:])
                 else:
@@ -52,9 +74,10 @@ def tile_lookup_pjsig_out_kernel(tc, z, wt, y, offs, out):
         for b in range(blocks):
             gate = held.tile([P, entries], F32, name=f"gate{b}")
             gated = held.tile([P, entries], F32, name=f"gated{b}")
-            for start in range(0, entries, PIECE):
-                piece = slice(start, start + PIECE)
-                listed = offsets[:, start // GROUP : (start + PIECE) // GROUP]
+            last = b == blocks - 1
+            for piece in (halving(entries, SMALLEST) if last else [slice(0, entries)]):
+                listed = offsets[:, piece.start // GROUP : piece.stop // GROUP]
                 nc.scalar.activation(gate[:, piece], table[b][:].indirect(listed), SIGMOID)
-                nc.vector.tensor_tensor(gated[:, piece], gate[:, piece], stream[b][:, piece], MULT)
+            for piece in halving(entries, SMALLEST if last else entries // 2):
+                nc.vector.tensor_tensor(gated[:, piece], gate[:, piece], stream[:, b, piece], MULT)
                 nc.sync.dma_start(out[b * P : (b + 1) * P, piece], gated[:, piece])

@@ -1,18 +1,22 @@
 import concourse.mybir as mybir
 
 P = 128
-BANK = 512
 GROUP = 16
-SMALLEST = 128
 BANKS = 8
+LOAD = 512
+STEP = 256
+SMALLEST = 128
 WARM_MATMULS = 6
-WARM_WIDTH = 256
 
 FLOPS = 2 * 256 * 256 * 2048
 
 BF16, F32, U16 = mybir.dt.bfloat16, mybir.dt.float32, mybir.dt.uint16
 SIGMOID = mybir.ActivationFunctionType.Sigmoid
 MULT = mybir.AluOpType.mult
+
+
+def cut(total, width):
+    return [slice(start, start + width) for start in range(0, total, width)]
 
 
 def halving(total, smallest):
@@ -29,8 +33,8 @@ def tile_lookup_pjsig_out_kernel(tc, z, wt, y, offs, out):
     features, places = z.shape
     rows, entries = y.shape
     halves, blocks = features // P, rows // P
-    edges = [0] + list(range(BANK // 2, places, BANK)) + [places]
-    chunks = [slice(lo, hi) for lo, hi in zip(edges, edges[1:])]
+    edges = [0] + list(range(STEP, places, LOAD)) + [places]
+    loads = [slice(lo, hi) for lo, hi in zip(edges, edges[1:])]
 
     z_split = z.rearrange("(p h) s -> p h s", h=halves)
     wt_split = wt.rearrange("(p h) r -> p h r", h=halves)
@@ -40,44 +44,44 @@ def tile_lookup_pjsig_out_kernel(tc, z, wt, y, offs, out):
         tc.psum_pool(name="psum", bufs=BANKS) as psum,
     ):
         weights = held.tile([P, halves, rows], BF16, name="weights")
-        nc.scalar.dma_start(weights[:], wt_split)
-        feats = held.tile([P, halves, places], BF16, name="feats")
-        for chunk in chunks:
-            nc.sync.dma_start(feats[:, :, chunk], z_split[:, :, chunk])
+        nc.scalar.dma_start(weights[:, :, 0:P], wt_split[:, :, 0:P])
+        feats = held.tile([P, halves, places], BF16, name="feats", tag="reused")
+        for load in loads:
+            nc.sync.dma_start(feats[:, :, load], z_split[:, :, load])
         offsets = held.tile([P, entries // GROUP], U16, name="offsets")
         nc.sync.dma_start(offsets[:], offs)
+        nc.sync.dma_start(weights[:, :, P:rows], wt_split[:, :, P:rows])
+        stream = held.tile([P, blocks, entries], F32, name="stream")
+        nc.sync.dma_start(stream[:], y.rearrange("(b p) j -> p b j", p=P))
 
-        zeros = held.tile([P, WARM_WIDTH], BF16, name="zeros", tag="late")
+        zeros = held.tile([P, STEP], BF16, name="zeros")
         nc.vector.memset(zeros[:], 0.0)
         unused_gate = held.tile([P, 1], F32, name="unused_gate")
         nc.scalar.activation(unused_gate[:], zeros[:, 0:1], SIGMOID)
-        unused_scores = psum.tile([P, WARM_WIDTH], F32, name="unused_scores", tag="bank")
+        unused_scores = psum.tile([P, STEP], F32, name="unused_scores", tag="bank")
         for w in range(WARM_MATMULS):
             nc.tensor.matmul(unused_scores[:], zeros[:, 0:P], zeros[:], start=True, stop=True)
 
-        stream = held.tile([P, blocks, entries], F32, name="stream", tag="late")
-        nc.sync.dma_start(stream[:], y.rearrange("(b p) j -> p b j", p=P))
-
         table = [held.tile([P, places], F32, name=f"table{b}") for b in range(blocks)]
         for b in range(blocks):
-            for c, chunk in enumerate(chunks):
-                scores = psum.tile([P, chunk.stop - chunk.start], F32, name=f"scores{b}_{c}", tag="bank")
+            for s, step in enumerate(cut(places, STEP)):
+                scores = psum.tile([P, STEP], F32, name=f"scores{b}_{s}", tag="bank")
                 for h in range(halves):
-                    nc.tensor.matmul(scores[:], weights[:, h, b * P : (b + 1) * P], feats[:, h, chunk],
+                    nc.tensor.matmul(scores[:], weights[:, h, b * P : (b + 1) * P], feats[:, h, step],
                                      start=(h == 0), stop=(h == halves - 1))
-                columns = table[b][:, chunk]
-                if b == 0 and c % 2 == 1:
-                    nc.scalar.copy(columns, scores[:])
+                if b == 0 and s % 2 == 1:
+                    nc.scalar.copy(table[b][:, step], scores[:])
                 else:
-                    nc.vector.tensor_copy(columns, scores[:])
+                    nc.vector.tensor_copy(table[b][:, step], scores[:])
 
+        gated = held.tile([P, blocks, entries], F32, name="gated", tag="reused")
         for b in range(blocks):
             gate = held.tile([P, entries], F32, name=f"gate{b}")
-            gated = held.tile([P, entries], F32, name=f"gated{b}")
             last = b == blocks - 1
-            for piece in (halving(entries, SMALLEST) if last else [slice(0, entries)]):
+            pieces = halving(entries, SMALLEST)
+            for piece in (pieces if last else cut(entries, entries)):
                 listed = offsets[:, piece.start // GROUP : piece.stop // GROUP]
                 nc.scalar.activation(gate[:, piece], table[b][:].indirect(listed), SIGMOID)
-            for piece in halving(entries, SMALLEST if last else entries // 2):
-                nc.vector.tensor_tensor(gated[:, piece], gate[:, piece], stream[:, b, piece], MULT)
-                nc.sync.dma_start(out[b * P : (b + 1) * P, piece], gated[:, piece])
+            for piece in (pieces if last else cut(entries, entries // 2)):
+                nc.vector.tensor_tensor(gated[:, b, piece], gate[:, piece], stream[:, b, piece], MULT)
+                nc.sync.dma_start(out[b * P : (b + 1) * P, piece], gated[:, b, piece])

@@ -3,9 +3,9 @@ import concourse.mybir as mybir
 P = 128
 GROUP = 16
 BANKS = 8
-LOAD = 512
+LOAD = 1024
 STEP = 256
-SMALLEST = 128
+PIECE = 256
 WARM_MATMULS = 6
 
 FLOPS = 2 * 256 * 256 * 2048
@@ -15,17 +15,8 @@ SIGMOID = mybir.ActivationFunctionType.Sigmoid
 MULT = mybir.AluOpType.mult
 
 
-def cut(total, width):
-    return [slice(start, start + width) for start in range(0, total, width)]
-
-
-def halving(total, smallest):
-    pieces, start = [], 0
-    while total - start > smallest:
-        width = (total - start) // 2
-        pieces.append(slice(start, start + width))
-        start += width
-    return pieces + [slice(start, total)]
+def cut(first, end, width):
+    return [slice(start, start + width) for start in range(first, end, width)]
 
 
 def tile_lookup_pjsig_out_kernel(tc, z, wt, y, offs, out):
@@ -33,8 +24,6 @@ def tile_lookup_pjsig_out_kernel(tc, z, wt, y, offs, out):
     features, places = z.shape
     rows, entries = y.shape
     halves, blocks = features // P, rows // P
-    edges = [0] + list(range(STEP, places, LOAD)) + [places]
-    loads = [slice(lo, hi) for lo, hi in zip(edges, edges[1:])]
 
     z_split = z.rearrange("(p h) s -> p h s", h=halves)
     wt_split = wt.rearrange("(p h) r -> p h r", h=halves)
@@ -46,8 +35,9 @@ def tile_lookup_pjsig_out_kernel(tc, z, wt, y, offs, out):
         weights = held.tile([P, halves, rows], BF16, name="weights")
         nc.scalar.dma_start(weights[:, :, 0:P], wt_split[:, :, 0:P])
         feats = held.tile([P, halves, places], BF16, name="feats", tag="reused")
-        for load in loads:
-            nc.sync.dma_start(feats[:, :, load], z_split[:, :, load])
+        for load in cut(0, places, LOAD):
+            for h in range(halves):
+                nc.sync.dma_start(feats[:, h, load], z_split[:, h, load])
         offsets = held.tile([P, entries // GROUP], U16, name="offsets")
         nc.sync.dma_start(offsets[:], offs)
         nc.sync.dma_start(weights[:, :, P:rows], wt_split[:, :, P:rows])
@@ -64,24 +54,28 @@ def tile_lookup_pjsig_out_kernel(tc, z, wt, y, offs, out):
 
         table = [held.tile([P, places], F32, name=f"table{b}") for b in range(blocks)]
         for b in range(blocks):
-            for s, step in enumerate(cut(places, STEP)):
-                scores = psum.tile([P, STEP], F32, name=f"scores{b}_{s}", tag="bank")
+            for span in cut(0, places, LOAD if b == 0 else STEP):
+                steps = cut(span.start, span.stop, STEP)
+                scores = [psum.tile([P, STEP], F32, name=f"scores{b}_{step.start}", tag="bank") for step in steps]
                 for h in range(halves):
-                    nc.tensor.matmul(scores[:], weights[:, h, b * P : (b + 1) * P], feats[:, h, step],
-                                     start=(h == 0), stop=(h == halves - 1))
-                if b == 0 and s % 2 == 1:
-                    nc.scalar.copy(table[b][:, step], scores[:])
-                else:
-                    nc.vector.tensor_copy(table[b][:, step], scores[:])
+                    for step, bank in zip(steps, scores):
+                        nc.tensor.matmul(bank[:], weights[:, h, b * P : (b + 1) * P], feats[:, h, step],
+                                         start=(h == 0), stop=(h == halves - 1))
+                for step, bank in zip(steps, scores):
+                    if b == 0 and (step.start // STEP) % 2 == 1:
+                        nc.scalar.copy(table[b][:, step], bank[:])
+                    else:
+                        nc.vector.tensor_copy(table[b][:, step], bank[:])
 
         gated = held.tile([P, blocks, entries], F32, name="gated", tag="reused")
         for b in range(blocks):
             gate = held.tile([P, entries], F32, name=f"gate{b}")
-            last = b == blocks - 1
-            pieces = halving(entries, SMALLEST)
-            for piece in (pieces if last else cut(entries, entries)):
+            if b < blocks - 1:
+                pieces = cut(0, entries, entries // 2)
+            else:
+                pieces = cut(0, entries - PIECE, PIECE) + cut(entries - PIECE, entries, PIECE // 2)
+            for piece in pieces:
                 listed = offsets[:, piece.start // GROUP : piece.stop // GROUP]
                 nc.scalar.activation(gate[:, piece], table[b][:].indirect(listed), SIGMOID)
-            for piece in (pieces if last else cut(entries, entries // 2)):
                 nc.vector.tensor_tensor(gated[:, b, piece], gate[:, piece], stream[:, b, piece], MULT)
                 nc.sync.dma_start(out[b * P : (b + 1) * P, piece], gated[:, b, piece])

import concourse.mybir as mybir

P = 128
GROUP = 16
BANKS = 8
LOAD = 1024
STEP = 256
PIECE = 256
WARM_MATMULS = 6

FLOPS = 2 * 256 * 256 * 2048

BF16, F32, U16 = mybir.dt.bfloat16, mybir.dt.float32, mybir.dt.uint16
SIGMOID = mybir.ActivationFunctionType.Sigmoid
MULT = mybir.AluOpType.mult


def cut(first, end, width):
    return [slice(start, start + width) for start in range(first, end, width)]


def tile_lookup_pjsig_out_kernel(tc, z, wt, y, offs, out):
    nc = tc.nc
    features, places = z.shape
    rows, entries = y.shape
    halves, blocks = features // P, rows // P

    z_split = z.rearrange("(p h) s -> p h s", h=halves)
    wt_split = wt.rearrange("(p h) r -> p h r", h=halves)

    with (
        tc.tile_pool(name="held", bufs=1) as held,
        tc.psum_pool(name="psum", bufs=BANKS) as psum,
    ):
        weights = held.tile([P, halves, rows], BF16, name="weights")
        nc.scalar.dma_start(weights[:, :, 0:P], wt_split[:, :, 0:P])
        feats = held.tile([P, halves, places], BF16, name="feats", tag="reused")
        for load in cut(0, places, LOAD):
            for h in range(halves):
                nc.sync.dma_start(feats[:, h, load], z_split[:, h, load])
        offsets = held.tile([P, entries // GROUP], U16, name="offsets")
        nc.sync.dma_start(offsets[:], offs)
        nc.sync.dma_start(weights[:, :, P:rows], wt_split[:, :, P:rows])
        stream = held.tile([P, blocks, entries], F32, name="stream")
        nc.sync.dma_start(stream[:], y.rearrange("(b p) j -> p b j", p=P))

        zeros = held.tile([P, STEP], BF16, name="zeros")
        nc.vector.memset(zeros[:], 0.0)
        unused_gate = held.tile([P, 1], F32, name="unused_gate")
        nc.scalar.activation(unused_gate[:], zeros[:, 0:1], SIGMOID)
        unused_scores = psum.tile([P, STEP], F32, name="unused_scores", tag="bank")
        for w in range(WARM_MATMULS):
            nc.tensor.matmul(unused_scores[:], zeros[:, 0:P], zeros[:], start=True, stop=True)

        table = [held.tile([P, places], F32, name=f"table{b}") for b in range(blocks)]
        for b in range(blocks):
            for span in cut(0, places, LOAD if b == 0 else STEP):
                steps = cut(span.start, span.stop, STEP)
                scores = [psum.tile([P, STEP], F32, name=f"scores{b}_{step.start}", tag="bank") for step in steps]
                for h in range(halves):
                    for step, bank in zip(steps, scores):
                        nc.tensor.matmul(bank[:], weights[:, h, b * P : (b + 1) * P], feats[:, h, step],
                                         start=(h == 0), stop=(h == halves - 1))
                for step, bank in zip(steps, scores):
                    if b == 0 and (step.start // STEP) % 2 == 1:
                        nc.scalar.copy(table[b][:, step], bank[:])
                    else:
                        nc.vector.tensor_copy(table[b][:, step], bank[:])

        gated = held.tile([P, blocks, entries], F32, name="gated", tag="reused")
        for b in range(blocks):
            gate = held.tile([P, entries], F32, name=f"gate{b}")
            if b < blocks - 1:
                pieces = cut(0, entries, entries // 2)
            else:
                pieces = cut(0, entries - PIECE, PIECE) + cut(entries - PIECE, entries, PIECE // 2)
            for piece in pieces:
                listed = offsets[:, piece.start // GROUP : piece.stop // GROUP]
                nc.scalar.activation(gate[:, piece], table[b][:].indirect(listed), SIGMOID)
                nc.vector.tensor_tensor(gated[:, b, piece], gate[:, piece], stream[:, b, piece], MULT)
                nc.sync.dma_start(out[b * P : (b + 1) * P, piece], gated[:, b, piece])
